import numpy as np
import ml_dtypes


def mxq(x, axis, fmt="e4m3"):
    dtype, down = {"e4m3": (ml_dtypes.float8_e4m3fn, 7), "e5m2": (ml_dtypes.float8_e5m2, 14)}[fmt]
    v = np.moveaxis(np.asarray(x, np.float32).astype(ml_dtypes.bfloat16).astype(np.float64), axis, -1)
    blocks = v.reshape(v.shape[:-1] + (-1, 32))
    amax = np.abs(blocks).max(-1, keepdims=True)
    byte = np.maximum(np.where(amax > 0, np.frexp(amax)[1] - 1 + 127, 0) - down, 1)
    scale = np.exp2(byte - 127.0)
    codes = (blocks / scale).astype(np.float32).astype(dtype).astype(np.float64)
    return np.moveaxis((codes * scale).reshape(v.shape), -1, axis)


WIDE = False


def mx_kscale(k):
    if not WIDE:
        return np.ones(k)
    levels = np.array([30, -30])
    if k % 512:
        return np.exp2(np.random.permutation(np.resize(levels, k // 32))).repeat(32)
    a = np.empty((k // 512, 16))
    for p in range(k // 512):
        a[p, :8] = np.random.permutation(np.resize(levels, 8))
        for g in range(8):
            far = levels[np.abs(levels - a[p, g]) >= 10]
            a[p, g + 8] = far[np.random.randint(len(far))]
    return np.exp2(a.ravel()).repeat(32)


def f64(x):
    return np.asarray(x).astype(np.float64)


def striped(idx):
    return np.tile(np.asarray(idx).reshape(-1, 16).T, (8, 1)).astype(np.uint16)


def unstriped(offs):
    return offs[:16].T.reshape(-1).astype(np.int64)


E2M1 = np.array([0.0, 0.5, 1.0, 1.5, 2.0, 3.0, 4.0, 6.0, -0.0, -0.5, -1.0, -1.5, -2.0, -3.0, -4.0, -6.0])


def pack_weight(w, fmt):
    k, n = w.shape
    w = f64(np.asarray(w, np.float32).astype(ml_dtypes.bfloat16)).reshape(k // 32, 32, n)
    amax = np.abs(w).max(1)
    if fmt in ("e4m3", "e5m2"):
        byte = np.frexp(amax)[1] - 1 + 127 - (7 if fmt == "e4m3" else 14)
    else:
        mant, ex = np.frexp(amax / 6.0)
        byte = np.where(mant > 0.5, ex, ex - 1) + 127
    byte = np.clip(np.where(amax > 0, byte, 1), 1, 254)
    scaled = (w * np.exp2(127.0 - byte)[:, None, :]).reshape(k, n).astype(np.float32)
    by_word = np.ascontiguousarray(scaled.reshape(k // 512, 128, 4, n).transpose(0, 1, 3, 2))
    if fmt in ("e4m3", "e5m2"):
        words = by_word.astype(ml_dtypes.float8_e4m3fn if fmt == "e4m3" else ml_dtypes.float8_e5m2).view(np.uint8)
    else:
        c = by_word.astype(ml_dtypes.float4_e2m1fn).view(np.uint8) & 0xF
        words = (c[..., 0::2] | (c[..., 1::2] << 4)).reshape(k // 512, 128, 2 * n)
    return np.ascontiguousarray(words), np.ascontiguousarray(byte.astype(np.uint8).reshape(k // 512, 16, n))


def unpack_weight(words, scales, fmt):
    g, _, n = scales.shape
    words = np.ascontiguousarray(words).reshape(g, 128, n, -1)
    if fmt in ("e4m3", "e5m2"):
        vals = words.view(ml_dtypes.float8_e4m3fn if fmt == "e4m3" else ml_dtypes.float8_e5m2).astype(np.float64)
    else:
        nib = np.empty((g, 128, n, 4), np.uint8)
        nib[..., 0::2] = words & 0xF
        nib[..., 1::2] = words >> 4
        vals = E2M1[nib]
    vals = vals * np.repeat(np.exp2(scales.astype(np.float64) - 127.0), 8, axis=1)[..., None]
    return vals.transpose(0, 1, 3, 2).reshape(g * 512, n)


def e4m3fn_bytes(y):
    return np.clip(np.asarray(y, np.float64), -448.0, 448.0).astype(np.float32).astype(ml_dtypes.float8_e4m3fn).view(np.uint8)


def e4m3fn_values(b):
    return np.asarray(b, np.uint8).view(ml_dtypes.float8_e4m3fn).astype(np.float64)


K, T, J, R, C, V, O, N = 512, 1024, 256, 512, 512, 1024, 256, 256


def setup_inputs():
    n = np.random.standard_normal
    idx = np.random.permutation(T)[:J]
    idx2 = np.random.permutation(C)[:J]
    idx3 = np.random.permutation(C)[:O]
    idx4 = np.random.permutation(V)[:O]
    fk = mx_kscale(K)
    fr = mx_kscale(R)
    xtp = pack_weight(n((K, T)) / fk[:, None], "e5m2")
    wp = pack_weight(n((K, R)) * 1 / np.sqrt(K) * fk[:, None] * fr, "e2m1")
    wbp = pack_weight(n((R, N)) * 1 / np.sqrt(R) / fr[:, None], "e2m1")
    return {
        "xt_words": xtp[0],
        "xt_scales": xtp[1],
        "w_words": wp[0],
        "w_scales": wp[1],
        "ca": e4m3fn_bytes(60.0 * n((R, V))),
        "st": (np.random.uniform(0.008, 0.024, (R, 1)) * fr[:, None]).astype(np.float32),
        "wb_words": wbp[0],
        "wb_scales": wbp[1],
        "offs": striped(idx),
        "offs2": striped(idx2),
        "offs3": striped(idx3),
        "offs4": striped(idx4),
    }


def reference(xt_words, xt_scales, w_words, w_scales, ca, st, wb_words, wb_scales, offs, offs2, offs3, offs4):
    idx = unstriped(offs)
    idx2 = unstriped(offs2)
    idx3 = unstriped(offs3)
    idx4 = unstriped(offs4)
    xtu = unpack_weight(xt_words, xt_scales, "e5m2")
    wu = unpack_weight(w_words, w_scales, "e2m1")
    wbu = unpack_weight(wb_words, wb_scales, "e2m1")
    xtidxg = xtu[:, idx]
    a = wu.T @ xtidxg
    pw = np.zeros((R, C))
    pw[:, idx2] = a
    g1 = e4m3fn_values(ca)[:, idx4] * f64(st)
    hid = np.maximum(pw[:, idx3] + g1, 0.0)
    hidq = mxq(hid, 0, "e4m3")
    p = wbu.T @ hidq
    return p

@@ -1,0 +1,181 @@
+from contextlib import ExitStack
+
+import concourse.mybir as mybir
+
+K, T, J, R, C, V, O, N = 512, 1024, 256, 512, 512, 1024, 256, 256
+FLOPS = 2 * K * R * J + 2 * R * N * O
+
+F32 = mybir.dt.float32
+BF16 = mybir.dt.bfloat16
+I32 = mybir.dt.int32
+U32 = mybir.dt.uint32
+U16 = mybir.dt.uint16
+U8 = mybir.dt.uint8
+FP8 = mybir.dt.float8_e4m3fn
+E4M3X4 = mybir.dt.float8_e4m3fn_x4
+E5M2X4 = mybir.dt.float8_e5m2_x4
+E2M1X4 = mybir.dt.float4_e2m1fn_x4
+ALU = mybir.AluOpType
+ACT = mybir.ActivationFunctionType
+
+P = 128
+PACK = 4
+QUADS = 4
+RELU_SPLIT = 160
+
+
+def load_scale_rows(queue, plane, scales):
+    for q in range(QUADS):
+        queue.dma_start(
+            out=plane[32 * q : 32 * q + 4, :].bitcast(I32),
+            in_=scales[0, 4 * q : 4 * q + 4, :].bitcast(I32),
+        )
+
+
+def tile_list_boardoffset_kernel(
+    tc, xt_words, xt_scales, w_words, w_scales, ca, st, wb_words, wb_scales, offs, offs2, offs3, offs4, out
+):
+    nc = tc.nc
+    with ExitStack() as ctx:
+        lists = ctx.enter_context(tc.tile_pool(name="lists", bufs=1))
+        sb = ctx.enter_context(tc.tile_pool(name="sb", bufs=1))
+        psum = ctx.enter_context(tc.psum_pool(name="psum", bufs=1))
+
+        w_plane_raw = sb.tile([P, R], U8, name="w_plane_raw", align_bytes=64)
+        xt_plane = sb.tile([P, T], U8, name="xt_plane", align_bytes=64)
+        wb_plane = sb.tile([P, N], U8, name="wb_plane", align_bytes=64)
+        nc.vector.memset(w_plane_raw[:].bitcast(I32), 0)
+        nc.vector.memset(xt_plane[:].bitcast(I32), 0)
+        nc.vector.memset(wb_plane[:].bitcast(I32), 0)
+
+        xt_tab = sb.tile([P, T], I32, name="xt_tab", align_bytes=64)
+        nc.sync.dma_start(out=xt_tab[:], in_=xt_words[0].rearrange("p c r -> p (c r)").bitcast(I32))
+        tok_list = lists.tile([P, J // 16], U16, name="tok_list")
+        nc.sync.dma_start(tok_list[:], offs)
+        w_raw = sb.tile([P, 2 * R], U8, name="w_raw", align_bytes=64)
+        nc.scalar.dma_start(out=w_raw[:].bitcast(I32), in_=w_words[0].bitcast(I32))
+        load_scale_rows(nc.scalar, w_plane_raw, w_scales)
+        load_scale_rows(nc.sync, xt_plane, xt_scales)
+
+        shift_list = lists.tile([P, O // 16], U16, name="shift_list")
+        nc.sync.dma_start(shift_list[:], offs4)
+        ca_rows = ca.rearrange("(p t) v -> p t v", t=PACK)
+        ca_tab = []
+        for t in range(PACK):
+            tab = sb.tile([P, V], U8, name="ca_tab%d" % t, align_bytes=64)
+            nc.sync.dma_start(out=tab[:], in_=ca_rows[:, t, :])
+            ca_tab.append(tab)
+        put_list = lists.tile([P, J // 16], U16, name="put_list")
+        nc.sync.dma_start(put_list[:], offs2)
+        step = sb.tile([P, PACK], F32, name="step")
+        nc.sync.dma_start(out=step[:], in_=st.rearrange("(p t) one -> p (t one)", t=PACK))
+        read_list = lists.tile([P, O // 16], U16, name="read_list")
+        nc.sync.dma_start(read_list[:], offs3)
+        wb_codes = sb.tile([P, 2 * N], U8, name="wb_codes", align_bytes=64)
+        nc.sync.dma_start(out=wb_codes[:].bitcast(I32), in_=wb_words[0].bitcast(I32))
+        load_scale_rows(nc.sync, wb_plane, wb_scales)
+
+        board = []
+        for t in range(PACK):
+            page = sb.tile([P, C], F32, name="board%d" % t, align_bytes=64)
+            nc.vector.memset(page[:], 0.0)
+            board.append(page)
+
+        w_codes = sb.tile([P, 2 * R], U8, name="w_codes", align_bytes=64)
+        nc.scalar.copy(
+            out=w_codes[:].bitcast(U16).rearrange("p (t m) -> p t m", t=PACK),
+            in_=w_raw[:].bitcast(U16).rearrange("p (m t) -> p t m", t=PACK),
+        )
+        w_plane = sb.tile([P, R], U8, name="w_plane", align_bytes=64)
+        nc.vector.tensor_copy(
+            out=w_plane[:].rearrange("p (t m) -> p t m", t=PACK),
+            in_=w_plane_raw[:].rearrange("p (m t) -> p t m", t=PACK),
+        )
+
+        x_codes = sb.tile([P, J], U32, name="x_codes", align_bytes=64)
+        nc.vector.tensor_copy(x_codes[:], xt_tab[:].bitcast(U32).indirect(tok_list[:]))
+        x_plane = sb.tile([P, J], U8, name="x_plane", align_bytes=64)
+        nc.vector.tensor_copy(x_plane[:], xt_plane[:].indirect(tok_list[:]))
+
+        a_sb = []
+        for t in range(PACK):
+            acc = psum.tile([P, J], F32, name="a_ps%d" % t)
+            nc.tensor.matmul_mx(
+                out=acc[:],
+                lhsT=w_codes[:, 2 * P * t : 2 * P * (t + 1)].bitcast(E2M1X4),
+                lhsT_scale=w_plane[:, P * t : P * (t + 1)],
+                rhs=x_codes[:].bitcast(E5M2X4),
+                rhs_scale=x_plane[:],
+                start=True,
+                stop=True,
+            )
+            a_sb.append((acc, sb.tile([P, J], F32, name="a_sb%d" % t, align_bytes=64)))
+
+        shift_codes = sb.tile([P, PACK, O], U8, name="shift_codes", align_bytes=64)
+        shift = sb.tile([P, PACK, O], F32, name="shift", align_bytes=64)
+        picked = sb.tile([P, PACK, O], F32, name="picked", align_bytes=64)
+        total = sb.tile([P, PACK, O], F32, name="total", align_bytes=64)
+
+        def look_up_shift(t):
+            nc.vector.tensor_copy(shift_codes[:, t, :], ca_tab[t][:].indirect(shift_list[:]))
+
+        def evacuate(t):
+            nc.scalar.copy(out=a_sb[t][1][:], in_=a_sb[t][0][:])
+
+        look_up_shift(0)
+        look_up_shift(1)
+        for t in (0, 2):
+            evacuate(t)
+            evacuate(t + 1)
+            nc.scalar.activation(out=board[t][:].indirect(put_list[:]), in_=a_sb[t][1][:], func=ACT.Copy)
+            nc.vector.tensor_copy(board[t + 1][:].indirect(put_list[:]), a_sb[t + 1][1][:])
+            look_up_shift(2 + t // 2)
+        for t in range(PACK):
+            nc.vector.tensor_scalar(
+                out=shift[:, t, :],
+                in0=shift_codes[:, t, :].bitcast(FP8),
+                scalar1=step[:, t : t + 1],
+                scalar2=None,
+                op0=ALU.mult,
+            )
+        for t in range(PACK):
+            nc.scalar.activation(out=picked[:, t, :], in_=board[t][:].indirect(read_list[:]), func=ACT.Copy)
+            nc.vector.tensor_tensor(out=total[:, t, :], in0=picked[:, t, :], in1=shift[:, t, :], op=ALU.add)
+
+        hid = sb.tile([P, O, PACK], BF16, name="hid", align_bytes=64)
+        lo, hi = slice(0, RELU_SPLIT), slice(RELU_SPLIT, O)
+        nc.vector.tensor_scalar(
+            out=hid[:, lo, :].rearrange("p (c i) t -> p c t i", i=4),
+            in0=total[:, :, lo].rearrange("p t (c i) -> p c t i", i=4),
+            scalar1=0.0,
+            scalar2=None,
+            op0=ALU.max,
+        )
+        nc.scalar.activation(
+            out=hid[:, hi, :].rearrange("p (c i) t -> p c t i", i=4),
+            in_=total[:, :, hi].rearrange("p t (c i) -> p c t i", i=4),
+            func=ACT.Relu,
+        )
+        h_codes = sb.tile([P, O], U32, name="h_codes", align_bytes=64)
+        h_plane = sb.tile([P, O], U8, name="h_plane", align_bytes=64)
+        nc.vector.quantize_mx(
+            out=h_codes[:].bitcast(E4M3X4), scales=h_plane[:], in_=hid[:].rearrange("p o t -> p (o t)")
+        )
+
+        for half, (engine, queue) in enumerate(((nc.vector, nc.sync), (nc.scalar, nc.scalar))):
+            acc = psum.tile([P, O], F32, name="out_ps%d" % half)
+            nc.tensor.matmul_mx(
+                out=acc[:],
+                lhsT=wb_codes[:, 2 * P * half : 2 * P * (half + 1)].bitcast(E2M1X4),
+                lhsT_scale=wb_plane[:, P * half : P * (half + 1)],
+                rhs=h_codes[:].bitcast(E4M3X4),
+                rhs_scale=h_plane[:],
+                start=True,
+                stop=True,
+            )
+            res = sb.tile([P, O], F32, name="res%d" % half, align_bytes=64)
+            if half == 0:
+                engine.tensor_copy(out=res[:], in_=acc[:])
+            else:
+                engine.copy(out=res[:], in_=acc[:])
+            queue.dma_start(out=out[P * half : P * (half + 1), :], in_=res[:])

@@ -21,7 +21,6 @@ ACT = mybir.ActivationFunctionType
 P = 128
 PACK = 4
 QUADS = 4
-RELU_SPLIT = 160
 
 
 def load_scale_rows(queue, plane, scales):
@@ -44,17 +43,18 @@ def tile_list_boardoffset_kernel(
         w_plane_raw = sb.tile([P, R], U8, name="w_plane_raw", align_bytes=64)
         xt_plane = sb.tile([P, T], U8, name="xt_plane", align_bytes=64)
         wb_plane = sb.tile([P, N], U8, name="wb_plane", align_bytes=64)
-        nc.vector.memset(w_plane_raw[:].bitcast(I32), 0)
         nc.vector.memset(xt_plane[:].bitcast(I32), 0)
+        nc.vector.memset(w_plane_raw[:].bitcast(I32), 0)
         nc.vector.memset(wb_plane[:].bitcast(I32), 0)
 
         xt_tab = sb.tile([P, T], I32, name="xt_tab", align_bytes=64)
-        nc.sync.dma_start(out=xt_tab[:], in_=xt_words[0].rearrange("p c r -> p (c r)").bitcast(I32))
         tok_list = lists.tile([P, J // 16], U16, name="tok_list")
         nc.sync.dma_start(tok_list[:], offs)
+        w_rows = sb.tile([4, QUADS, R // 4], I32, name="w_rows", align_bytes=64)
+        nc.scalar.dma_start(out=w_rows[:], in_=w_scales[0].bitcast(I32).rearrange("(q r) c -> r q c", q=QUADS))
+        nc.sync.dma_start(out=xt_tab[:], in_=xt_words[0].rearrange("p c r -> p (c r)").bitcast(I32))
         w_raw = sb.tile([P, 2 * R], U8, name="w_raw", align_bytes=64)
         nc.scalar.dma_start(out=w_raw[:].bitcast(I32), in_=w_words[0].bitcast(I32))
-        load_scale_rows(nc.scalar, w_plane_raw, w_scales)
         load_scale_rows(nc.sync, xt_plane, xt_scales)
 
         shift_list = lists.tile([P, O // 16], U16, name="shift_list")
@@ -62,7 +62,7 @@ def tile_list_boardoffset_kernel(
         ca_rows = ca.rearrange("(p t) v -> p t v", t=PACK)
         ca_tab = []
         for t in range(PACK):
-            tab = sb.tile([P, V], U8, name="ca_tab%d" % t, align_bytes=64)
+            tab = sb.tile([P, V], U8, name="ca_tab%d" % t, tag="ca_tab%d" % t, align_bytes=64)
             nc.sync.dma_start(out=tab[:], in_=ca_rows[:, t, :])
             ca_tab.append(tab)
         put_list = lists.tile([P, J // 16], U16, name="put_list")
@@ -86,6 +86,8 @@ def tile_list_boardoffset_kernel(
             out=w_codes[:].bitcast(U16).rearrange("p (t m) -> p t m", t=PACK),
             in_=w_raw[:].bitcast(U16).rearrange("p (m t) -> p t m", t=PACK),
         )
+        for q in range(QUADS):
+            nc.vector.tensor_copy(out=w_plane_raw[32 * q : 32 * q + 4, :].bitcast(I32), in_=w_rows[:, q, :])
         w_plane = sb.tile([P, R], U8, name="w_plane", align_bytes=64)
         nc.vector.tensor_copy(
             out=w_plane[:].rearrange("p (t m) -> p t m", t=PACK),
@@ -97,8 +99,8 @@ def tile_list_boardoffset_kernel(
         x_plane = sb.tile([P, J], U8, name="x_plane", align_bytes=64)
         nc.vector.tensor_copy(x_plane[:], xt_plane[:].indirect(tok_list[:]))
 
-        a_sb = []
-        for t in range(PACK):
+        a_sb = {}
+        for t in (0, 1, 3, 2):
             acc = psum.tile([P, J], F32, name="a_ps%d" % t)
             nc.tensor.matmul_mx(
                 out=acc[:],
@@ -109,27 +111,30 @@ def tile_list_boardoffset_kernel(
                 start=True,
                 stop=True,
             )
-            a_sb.append((acc, sb.tile([P, J], F32, name="a_sb%d" % t, align_bytes=64)))
+            tag = "ca_tab1" if t == 1 else "a_sb%d" % t
+            a_sb[t] = (acc, sb.tile([P, J], F32, name="a_sb%d" % t, tag=tag, align_bytes=64))
 
         shift_codes = sb.tile([P, PACK, O], U8, name="shift_codes", align_bytes=64)
-        shift = sb.tile([P, PACK, O], F32, name="shift", align_bytes=64)
-        picked = sb.tile([P, PACK, O], F32, name="picked", align_bytes=64)
-        total = sb.tile([P, PACK, O], F32, name="total", align_bytes=64)
+        shift = sb.tile([P, PACK, O], F32, name="shift", tag="ca_tab1", align_bytes=64)
 
         def look_up_shift(t):
             nc.vector.tensor_copy(shift_codes[:, t, :], ca_tab[t][:].indirect(shift_list[:]))
 
-        def evacuate(t):
-            nc.scalar.copy(out=a_sb[t][1][:], in_=a_sb[t][0][:])
+        def put(engine, t, lo, hi):
+            window = board[t][:].indirect(put_list[:, lo // 16 : hi // 16])
+            if engine is nc.scalar:
+                nc.scalar.activation(out=window, in_=a_sb[t][1][:, lo:hi], func=ACT.Copy)
+            else:
+                nc.vector.tensor_copy(window, a_sb[t][1][:, lo:hi])
 
-        look_up_shift(0)
-        look_up_shift(1)
-        for t in (0, 2):
-            evacuate(t)
-            evacuate(t + 1)
-            nc.scalar.activation(out=board[t][:].indirect(put_list[:]), in_=a_sb[t][1][:], func=ACT.Copy)
-            nc.vector.tensor_copy(board[t + 1][:].indirect(put_list[:]), a_sb[t + 1][1][:])
-            look_up_shift(2 + t // 2)
+        for t in range(PACK):
+            look_up_shift(t)
+        for t in (0, 1, 3, 2):
+            nc.scalar.copy(out=a_sb[t][1][:], in_=a_sb[t][0][:])
+        put(nc.scalar, 0, 0, J)
+        put(nc.vector, 1, 0, J)
+        put(nc.scalar, 2, 0, J)
+        put(nc.vector, 3, 0, J)
         for t in range(PACK):
             nc.vector.tensor_scalar(
                 out=shift[:, t, :],
@@ -138,44 +143,66 @@ def tile_list_boardoffset_kernel(
                 scalar2=None,
                 op0=ALU.mult,
             )
-        for t in range(PACK):
-            nc.scalar.activation(out=picked[:, t, :], in_=board[t][:].indirect(read_list[:]), func=ACT.Copy)
-            nc.vector.tensor_tensor(out=total[:, t, :], in0=picked[:, t, :], in1=shift[:, t, :], op=ALU.add)
+        H = O // 2
+        picked = [sb.tile([P, PACK - 1, H], F32, name="picked%d" % h, align_bytes=64) for h in range(2)]
+        total = [sb.tile([P, PACK, H], F32, name="total%d" % h, align_bytes=64) for h in range(2)]
+        hid = [sb.tile([P, H, PACK], BF16, name="hid%d" % h, align_bytes=64) for h in range(2)]
+        h_codes = [sb.tile([P, H], U32, name="h_codes%d" % h, align_bytes=64) for h in range(2)]
+        h_plane = [sb.tile([P, H], U8, name="h_plane%d" % h, align_bytes=64) for h in range(2)]
+        for h in range(2):
+            places = read_list[:, h * H // 16 : (h + 1) * H // 16]
+            cols = slice(h * H, (h + 1) * H)
+            for t in range(PACK - 1):
+                nc.scalar.activation(out=picked[h][:, t, :], in_=board[t][:].indirect(places), func=ACT.Copy)
+            nc.vector.tensor_tensor(
+                out=total[h][:, 3, :], in0=board[3][:].indirect(places), in1=shift[:, 3, cols], op=ALU.add
+            )
+            nc.vector.tensor_tensor(out=total[h][:, 0:3, :], in0=picked[h][:], in1=shift[:, 0:3, cols], op=ALU.add)
 
-        hid = sb.tile([P, O, PACK], BF16, name="hid", align_bytes=64)
-        lo, hi = slice(0, RELU_SPLIT), slice(RELU_SPLIT, O)
+        def quantise(h):
+            nc.vector.quantize_mx(
+                out=h_codes[h][:].bitcast(E4M3X4), scales=h_plane[h][:], in_=hid[h][:].rearrange("p o t -> p (o t)")
+            )
+
+        def multiply(h, half, acc):
+            nc.tensor.matmul_mx(
+                out=acc,
+                lhsT=wb_codes[:, 2 * P * half : 2 * P * (half + 1)].bitcast(E2M1X4),
+                lhsT_scale=wb_plane[:, P * half : P * (half + 1)],
+                rhs=h_codes[h][:].bitcast(E4M3X4),
+                rhs_scale=h_plane[h][:],
+                start=True,
+                stop=True,
+            )
+
+        nc.scalar.activation(
+            out=hid[0][:],
+            in_=total[0][:].rearrange("p t o -> p o t"),
+            func=ACT.Relu,
+        )
+        quantise(0)
         nc.vector.tensor_scalar(
-            out=hid[:, lo, :].rearrange("p (c i) t -> p c t i", i=4),
-            in0=total[:, :, lo].rearrange("p t (c i) -> p c t i", i=4),
+            out=hid[1][:],
+            in0=total[1][:].rearrange("p t o -> p o t"),
             scalar1=0.0,
             scalar2=None,
             op0=ALU.max,
         )
-        nc.scalar.activation(
-            out=hid[:, hi, :].rearrange("p (c i) t -> p c t i", i=4),
-            in_=total[:, :, hi].rearrange("p t (c i) -> p c t i", i=4),
-            func=ACT.Relu,
-        )
-        h_codes = sb.tile([P, O], U32, name="h_codes", align_bytes=64)
-        h_plane = sb.tile([P, O], U8, name="h_plane", align_bytes=64)
-        nc.vector.quantize_mx(
-            out=h_codes[:].bitcast(E4M3X4), scales=h_plane[:], in_=hid[:].rearrange("p o t -> p (o t)")
-        )
+        quantise(1)
 
-        for half, (engine, queue) in enumerate(((nc.vector, nc.sync), (nc.scalar, nc.scalar))):
-            acc = psum.tile([P, O], F32, name="out_ps%d" % half)
-            nc.tensor.matmul_mx(
-                out=acc[:],
-                lhsT=wb_codes[:, 2 * P * half : 2 * P * (half + 1)].bitcast(E2M1X4),
-                lhsT_scale=wb_plane[:, P * half : P * (half + 1)],
-                rhs=h_codes[:].bitcast(E4M3X4),
-                rhs_scale=h_plane[:],
-                start=True,
-                stop=True,
-            )
-            res = sb.tile([P, O], F32, name="res%d" % half, align_bytes=64)
+        acc0 = psum.tile([P, 2, H], F32, name="out_ps0")
+        for half in range(2):
+            multiply(0, half, acc0[:, half, :])
+        res0 = sb.tile([P, 2, H], F32, name="res0", align_bytes=64)
+        nc.scalar.copy(out=res0[:], in_=acc0[:])
+        nc.sync.dma_start(out=out[:, 0:H].rearrange("(half p) o -> p half o", half=2), in_=res0[:])
+        for half in range(2):
+            acc = psum.tile([P, H], F32, name="out_ps1%d" % half)
+            multiply(1, half, acc[:])
+            res = sb.tile([P, H], F32, name="res1%d" % half, align_bytes=64)
             if half == 0:
-                engine.tensor_copy(out=res[:], in_=acc[:])
+                nc.vector.tensor_copy(out=res[:], in_=acc[:])
+                nc.sync.dma_start(out=out[0:P, H:O], in_=res[:])
             else:
-                engine.copy(out=res[:], in_=acc[:])
-            queue.dma_start(out=out[P * half : P * (half + 1), :], in_=res[:])
+                nc.scalar.copy(out=res[:], in_=acc[:])
+                nc.scalar.dma_start(out=out[P:N, H:O], in_=res[:])

@@ -89,7 +89,7 @@ def tile_list_boardoffset_kernel(
         for q in range(QUADS):
             nc.vector.tensor_copy(out=w_plane_raw[32 * q : 32 * q + 4, :].bitcast(I32), in_=w_rows[:, q, :])
         w_plane = sb.tile([P, R], U8, name="w_plane", align_bytes=64)
-        nc.vector.tensor_copy(
+        nc.gpsimd.tensor_copy(
             out=w_plane[:].rearrange("p (t m) -> p t m", t=PACK),
             in_=w_plane_raw[:].rearrange("p (m t) -> p t m", t=PACK),
         )
@@ -115,7 +115,9 @@ def tile_list_boardoffset_kernel(
             a_sb[t] = (acc, sb.tile([P, J], F32, name="a_sb%d" % t, tag=tag, align_bytes=64))
 
         shift_codes = sb.tile([P, PACK, O], U8, name="shift_codes", align_bytes=64)
-        shift = sb.tile([P, PACK, O], F32, name="shift", tag="ca_tab1", align_bytes=64)
+        shift = sb.tile([P, PACK - 1, O], F32, name="shift", align_bytes=64)
+        values = sb.tile([P, PACK - 1, O], F32, name="values", align_bytes=64)
+        shift_last = sb.tile([P, O], F32, name="shift_last", tag="ca_tab1", align_bytes=64)
 
         def look_up_shift(t):
             nc.vector.tensor_copy(shift_codes[:, t, :], ca_tab[t][:].indirect(shift_list[:]))
@@ -127,22 +129,24 @@ def tile_list_boardoffset_kernel(
             else:
                 nc.vector.tensor_copy(window, a_sb[t][1][:, lo:hi])
 
-        for t in range(PACK):
+        for t in range(PACK - 1):
             look_up_shift(t)
-        for t in (0, 1, 3, 2):
+        nc.vector.tensor_copy(out=a_sb[1][1][:], in_=a_sb[1][0][:])
+        look_up_shift(3)
+        for t in (0, 3, 2):
             nc.scalar.copy(out=a_sb[t][1][:], in_=a_sb[t][0][:])
         put(nc.scalar, 0, 0, J)
         put(nc.vector, 1, 0, J)
         put(nc.scalar, 2, 0, J)
         put(nc.vector, 3, 0, J)
-        for t in range(PACK):
-            nc.vector.tensor_scalar(
-                out=shift[:, t, :],
-                in0=shift_codes[:, t, :].bitcast(FP8),
-                scalar1=step[:, t : t + 1],
-                scalar2=None,
-                op0=ALU.mult,
+        for t in range(PACK - 1):
+            nc.gpsimd.tensor_copy(out=values[:, t, :], in_=shift_codes[:, t, :].bitcast(FP8))
+            nc.gpsimd.tensor_scalar(
+                out=shift[:, t, :], in0=values[:, t, :], scalar1=step[:, t : t + 1], scalar2=0.0, op0=ALU.mult, op1=ALU.add
             )
+        nc.vector.tensor_scalar(
+            out=shift_last[:], in0=shift_codes[:, 3, :].bitcast(FP8), scalar1=step[:, 3:4], scalar2=None, op0=ALU.mult
+        )
         H = O // 2
         picked = [sb.tile([P, PACK - 1, H], F32, name="picked%d" % h, align_bytes=64) for h in range(2)]
         total = [sb.tile([P, PACK, H], F32, name="total%d" % h, align_bytes=64) for h in range(2)]
@@ -152,12 +156,15 @@ def tile_list_boardoffset_kernel(
         for h in range(2):
             places = read_list[:, h * H // 16 : (h + 1) * H // 16]
             cols = slice(h * H, (h + 1) * H)
-            for t in range(PACK - 1):
+            plain = PACK - 1
+            for t in range(plain):
                 nc.scalar.activation(out=picked[h][:, t, :], in_=board[t][:].indirect(places), func=ACT.Copy)
             nc.vector.tensor_tensor(
-                out=total[h][:, 3, :], in0=board[3][:].indirect(places), in1=shift[:, 3, cols], op=ALU.add
+                out=total[h][:, 3, :], in0=board[3][:].indirect(places), in1=shift_last[:, cols], op=ALU.add
             )
-            nc.vector.tensor_tensor(out=total[h][:, 0:3, :], in0=picked[h][:], in1=shift[:, 0:3, cols], op=ALU.add)
+            nc.vector.tensor_tensor(
+                out=total[h][:, 0:plain, :], in0=picked[h][:], in1=shift[:, 0:plain, cols], op=ALU.add
+            )
 
         def quantise(h):
             nc.vector.quantize_mx(

from contextlib import ExitStack

import concourse.mybir as mybir

K, T, J, R, C, V, O, N = 512, 1024, 256, 512, 512, 1024, 256, 256
FLOPS = 2 * K * R * J + 2 * R * N * O

F32 = mybir.dt.float32
BF16 = mybir.dt.bfloat16
I32 = mybir.dt.int32
U32 = mybir.dt.uint32
U16 = mybir.dt.uint16
U8 = mybir.dt.uint8
FP8 = mybir.dt.float8_e4m3fn
E4M3X4 = mybir.dt.float8_e4m3fn_x4
E5M2X4 = mybir.dt.float8_e5m2_x4
E2M1X4 = mybir.dt.float4_e2m1fn_x4
ALU = mybir.AluOpType
ACT = mybir.ActivationFunctionType

P = 128
PACK = 4
QUADS = 4


def load_scale_rows(queue, plane, scales):
    for q in range(QUADS):
        queue.dma_start(
            out=plane[32 * q : 32 * q + 4, :].bitcast(I32),
            in_=scales[0, 4 * q : 4 * q + 4, :].bitcast(I32),
        )


def tile_list_boardoffset_kernel(
    tc, xt_words, xt_scales, w_words, w_scales, ca, st, wb_words, wb_scales, offs, offs2, offs3, offs4, out
):
    nc = tc.nc
    with ExitStack() as ctx:
        lists = ctx.enter_context(tc.tile_pool(name="lists", bufs=1))
        sb = ctx.enter_context(tc.tile_pool(name="sb", bufs=1))
        psum = ctx.enter_context(tc.psum_pool(name="psum", bufs=1))

        w_plane_raw = sb.tile([P, R], U8, name="w_plane_raw", align_bytes=64)
        xt_plane = sb.tile([P, T], U8, name="xt_plane", align_bytes=64)
        wb_plane = sb.tile([P, N], U8, name="wb_plane", align_bytes=64)
        nc.vector.memset(xt_plane[:].bitcast(I32), 0)
        nc.vector.memset(w_plane_raw[:].bitcast(I32), 0)
        nc.vector.memset(wb_plane[:].bitcast(I32), 0)

        xt_tab = sb.tile([P, T], I32, name="xt_tab", align_bytes=64)
        tok_list = lists.tile([P, J // 16], U16, name="tok_list")
        nc.sync.dma_start(tok_list[:], offs)
        w_rows = sb.tile([4, QUADS, R // 4], I32, name="w_rows", align_bytes=64)
        nc.scalar.dma_start(out=w_rows[:], in_=w_scales[0].bitcast(I32).rearrange("(q r) c -> r q c", q=QUADS))
        nc.sync.dma_start(out=xt_tab[:], in_=xt_words[0].rearrange("p c r -> p (c r)").bitcast(I32))
        w_raw = sb.tile([P, 2 * R], U8, name="w_raw", align_bytes=64)
        nc.scalar.dma_start(out=w_raw[:].bitcast(I32), in_=w_words[0].bitcast(I32))
        load_scale_rows(nc.sync, xt_plane, xt_scales)

        shift_list = lists.tile([P, O // 16], U16, name="shift_list")
        nc.sync.dma_start(shift_list[:], offs4)
        ca_rows = ca.rearrange("(p t) v -> p t v", t=PACK)
        ca_tab = []
        for t in range(PACK):
            tab = sb.tile([P, V], U8, name="ca_tab%d" % t, tag="ca_tab%d" % t, align_bytes=64)
            nc.sync.dma_start(out=tab[:], in_=ca_rows[:, t, :])
            ca_tab.append(tab)
        put_list = lists.tile([P, J // 16], U16, name="put_list")
        nc.sync.dma_start(put_list[:], offs2)
        step = sb.tile([P, PACK], F32, name="step")
        nc.sync.dma_start(out=step[:], in_=st.rearrange("(p t) one -> p (t one)", t=PACK))
        read_list = lists.tile([P, O // 16], U16, name="read_list")
        nc.sync.dma_start(read_list[:], offs3)
        wb_codes = sb.tile([P, 2 * N], U8, name="wb_codes", align_bytes=64)
        nc.sync.dma_start(out=wb_codes[:].bitcast(I32), in_=wb_words[0].bitcast(I32))
        load_scale_rows(nc.sync, wb_plane, wb_scales)

        board = []
        for t in range(PACK):
            page = sb.tile([P, C], F32, name="board%d" % t, align_bytes=64)
            nc.vector.memset(page[:], 0.0)
            board.append(page)

        w_codes = sb.tile([P, 2 * R], U8, name="w_codes", align_bytes=64)
        nc.scalar.copy(
            out=w_codes[:].bitcast(U16).rearrange("p (t m) -> p t m", t=PACK),
            in_=w_raw[:].bitcast(U16).rearrange("p (m t) -> p t m", t=PACK),
        )
        for q in range(QUADS):
            nc.vector.tensor_copy(out=w_plane_raw[32 * q : 32 * q + 4, :].bitcast(I32), in_=w_rows[:, q, :])
        w_plane = sb.tile([P, R], U8, name="w_plane", align_bytes=64)
        nc.gpsimd.tensor_copy(
            out=w_plane[:].rearrange("p (t m) -> p t m", t=PACK),
            in_=w_plane_raw[:].rearrange("p (m t) -> p t m", t=PACK),
        )

        x_codes = sb.tile([P, J], U32, name="x_codes", align_bytes=64)
        nc.vector.tensor_copy(x_codes[:], xt_tab[:].bitcast(U32).indirect(tok_list[:]))
        x_plane = sb.tile([P, J], U8, name="x_plane", align_bytes=64)
        nc.vector.tensor_copy(x_plane[:], xt_plane[:].indirect(tok_list[:]))

        a_sb = {}
        for t in (0, 1, 3, 2):
            acc = psum.tile([P, J], F32, name="a_ps%d" % t)
            nc.tensor.matmul_mx(
                out=acc[:],
                lhsT=w_codes[:, 2 * P * t : 2 * P * (t + 1)].bitcast(E2M1X4),
                lhsT_scale=w_plane[:, P * t : P * (t + 1)],
                rhs=x_codes[:].bitcast(E5M2X4),
                rhs_scale=x_plane[:],
                start=True,
                stop=True,
            )
            tag = "ca_tab1" if t == 1 else "a_sb%d" % t
            a_sb[t] = (acc, sb.tile([P, J], F32, name="a_sb%d" % t, tag=tag, align_bytes=64))

        shift_codes = sb.tile([P, PACK, O], U8, name="shift_codes", align_bytes=64)
        shift = sb.tile([P, PACK - 1, O], F32, name="shift", align_bytes=64)
        values = sb.tile([P, PACK - 1, O], F32, name="values", align_bytes=64)
        shift_last = sb.tile([P, O], F32, name="shift_last", tag="ca_tab1", align_bytes=64)

        def look_up_shift(t):
            nc.vector.tensor_copy(shift_codes[:, t, :], ca_tab[t][:].indirect(shift_list[:]))

        def put(engine, t, lo, hi):
            window = board[t][:].indirect(put_list[:, lo // 16 : hi // 16])
            if engine is nc.scalar:
                nc.scalar.activation(out=window, in_=a_sb[t][1][:, lo:hi], func=ACT.Copy)
            else:
                nc.vector.tensor_copy(window, a_sb[t][1][:, lo:hi])

        for t in range(PACK - 1):
            look_up_shift(t)
        nc.vector.tensor_copy(out=a_sb[1][1][:], in_=a_sb[1][0][:])
        look_up_shift(3)
        for t in (0, 3, 2):
            nc.scalar.copy(out=a_sb[t][1][:], in_=a_sb[t][0][:])
        put(nc.scalar, 0, 0, J)
        put(nc.vector, 1, 0, J)
        put(nc.scalar, 2, 0, J)
        put(nc.vector, 3, 0, J)
        for t in range(PACK - 1):
            nc.gpsimd.tensor_copy(out=values[:, t, :], in_=shift_codes[:, t, :].bitcast(FP8))
            nc.gpsimd.tensor_scalar(
                out=shift[:, t, :], in0=values[:, t, :], scalar1=step[:, t : t + 1], scalar2=0.0, op0=ALU.mult, op1=ALU.add
            )
        nc.vector.tensor_scalar(
            out=shift_last[:], in0=shift_codes[:, 3, :].bitcast(FP8), scalar1=step[:, 3:4], scalar2=None, op0=ALU.mult
        )
        H = O // 2
        picked = [sb.tile([P, PACK - 1, H], F32, name="picked%d" % h, align_bytes=64) for h in range(2)]
        total = [sb.tile([P, PACK, H], F32, name="total%d" % h, align_bytes=64) for h in range(2)]
        hid = [sb.tile([P, H, PACK], BF16, name="hid%d" % h, align_bytes=64) for h in range(2)]
        h_codes = [sb.tile([P, H], U32, name="h_codes%d" % h, align_bytes=64) for h in range(2)]
        h_plane = [sb.tile([P, H], U8, name="h_plane%d" % h, align_bytes=64) for h in range(2)]
        for h in range(2):
            places = read_list[:, h * H // 16 : (h + 1) * H // 16]
            cols = slice(h * H, (h + 1) * H)
            plain = PACK - 1
            for t in range(plain):
                nc.scalar.activation(out=picked[h][:, t, :], in_=board[t][:].indirect(places), func=ACT.Copy)
            nc.vector.tensor_tensor(
                out=total[h][:, 3, :], in0=board[3][:].indirect(places), in1=shift_last[:, cols], op=ALU.add
            )
            nc.vector.tensor_tensor(
                out=total[h][:, 0:plain, :], in0=picked[h][:], in1=shift[:, 0:plain, cols], op=ALU.add
            )

        def quantise(h):
            nc.vector.quantize_mx(
                out=h_codes[h][:].bitcast(E4M3X4), scales=h_plane[h][:], in_=hid[h][:].rearrange("p o t -> p (o t)")
            )

        def multiply(h, half, acc):
            nc.tensor.matmul_mx(
                out=acc,
                lhsT=wb_codes[:, 2 * P * half : 2 * P * (half + 1)].bitcast(E2M1X4),
                lhsT_scale=wb_plane[:, P * half : P * (half + 1)],
                rhs=h_codes[h][:].bitcast(E4M3X4),
                rhs_scale=h_plane[h][:],
                start=True,
                stop=True,
            )

        nc.scalar.activation(
            out=hid[0][:],
            in_=total[0][:].rearrange("p t o -> p o t"),
            func=ACT.Relu,
        )
        quantise(0)
        nc.vector.tensor_scalar(
            out=hid[1][:],
            in0=total[1][:].rearrange("p t o -> p o t"),
            scalar1=0.0,
            scalar2=None,
            op0=ALU.max,
        )
        quantise(1)

        acc0 = psum.tile([P, 2, H], F32, name="out_ps0")
        for half in range(2):
            multiply(0, half, acc0[:, half, :])
        res0 = sb.tile([P, 2, H], F32, name="res0", align_bytes=64)
        nc.scalar.copy(out=res0[:], in_=acc0[:])
        nc.sync.dma_start(out=out[:, 0:H].rearrange("(half p) o -> p half o", half=2), in_=res0[:])
        for half in range(2):
            acc = psum.tile([P, H], F32, name="out_ps1%d" % half)
            multiply(1, half, acc[:])
            res = sb.tile([P, H], F32, name="res1%d" % half, align_bytes=64)
            if half == 0:
                nc.vector.tensor_copy(out=res[:], in_=acc[:])
                nc.sync.dma_start(out=out[0:P, H:O], in_=res[:])
            else:
                nc.scalar.copy(out=res[:], in_=acc[:])
                nc.scalar.dma_start(out=out[P:N, H:O], in_=res[:])
